import numpy as np
import ml_dtypes


def mxq(x, axis, fmt="e4m3"):
    dtype, down = {"e4m3": (ml_dtypes.float8_e4m3fn, 7), "e5m2": (ml_dtypes.float8_e5m2, 14)}[fmt]
    v = np.moveaxis(np.asarray(x, np.float32).astype(ml_dtypes.bfloat16).astype(np.float64), axis, -1)
    blocks = v.reshape(v.shape[:-1] + (-1, 32))
    amax = np.abs(blocks).max(-1, keepdims=True)
    byte = np.maximum(np.where(amax > 0, np.frexp(amax)[1] - 1 + 127, 0) - down, 1)
    scale = np.exp2(byte - 127.0)
    codes = (blocks / scale).astype(np.float32).astype(dtype).astype(np.float64)
    return np.moveaxis((codes * scale).reshape(v.shape), -1, axis)


WIDE = False


def mx_kscale(k):
    if not WIDE:
        return np.ones(k)
    levels = np.array([10, -10, 5, -5, 0])
    if k % 512:
        return np.exp2(np.random.permutation(np.resize(levels, k // 32))).repeat(32)
    a = np.empty((k // 512, 16))
    for p in range(k // 512):
        a[p, :8] = np.random.permutation(np.resize(levels, 8))
        for g in range(8):
            far = levels[np.abs(levels - a[p, g]) >= 10]
            a[p, g + 8] = far[np.random.randint(len(far))]
    return np.exp2(a.ravel()).repeat(32)


def f64(x):
    return np.asarray(x).astype(np.float64)


def striped(idx):
    return np.tile(idx.reshape(-1, 16).T, (8, 1)).astype(np.uint16)


def unstriped(offs):
    return offs[:16].T.reshape(-1).astype(np.int64)


def pack_weight(w):
    k, n = w.shape
    w = f64(np.asarray(w, np.float32).astype(ml_dtypes.bfloat16)).reshape(k // 32, 32, n)
    amax = np.abs(w).max(1)
    byte = np.clip(np.where(amax > 0, np.frexp(amax)[1] - 1 + 127 - 7, 1), 1, 254)
    scaled = (w * np.exp2(127.0 - byte)[:, None, :]).reshape(k, n).astype(np.float32)
    words = np.ascontiguousarray(scaled.reshape(k // 512, 128, 4, n).transpose(0, 1, 3, 2)).astype(ml_dtypes.float8_e4m3fn).view(np.uint8)
    return words, np.ascontiguousarray(byte.astype(np.uint8).reshape(k // 512, 16, n))


def unpack_weight(words, scales):
    g, p, n, _ = words.shape
    vals = np.ascontiguousarray(words).view(ml_dtypes.float8_e4m3fn).astype(np.float64) * np.repeat(np.exp2(scales.astype(np.float64) - 127.0), 8, axis=1)[..., None]
    return vals.transpose(0, 1, 3, 2).reshape(g * 512, n)


def relu2(v):
    return np.maximum(v, 0.0) ** 2


K, T, E, C, N = 512, 3072, 8, 256, 512


def by_expert(wq, xq):
    return np.concatenate([wq[e].T @ xq[:, e * C:(e + 1) * C] for e in range(E)], axis=1)


def setup_inputs():
    n = np.random.standard_normal
    s = mx_kscale(K)[:, None]
    packed = [pack_weight(m) for m in n((E, K, N)) / np.sqrt(K) / s[None]]
    return {
        "xT": (n((K, T)) * s).astype(np.float32),
        "w_words": np.stack([m[0] for m in packed]),
        "w_scales": np.stack([m[1] for m in packed]),
        "b": (0.3 * n((N, E))).astype(np.float32),
        "gate": np.tile(np.random.uniform(0.2, 1.0, E * C), (N, 1)).astype(np.float32),
        "offs": striped(np.random.permutation(T)[:E * C]),
    }


def reference(xT, w_words, w_scales, b, gate, offs):
    idx = unstriped(offs)
    xq = mxq(f64(xT)[:, idx], 0, "e4m3")
    w = np.stack([unpack_weight(w_words[e], w_scales[e]) for e in range(E)])
    y = by_expert(w, xq)
    y = relu2(y + np.repeat(f64(b), C, axis=1))
    out = np.zeros((N, T))
    out[:, idx] = f64(gate) * y
    return out

@@ -1,0 +1,108 @@
+from contextlib import ExitStack
+
+import concourse.mybir as mybir
+
+K, T, E, C, N = 512, 3072, 8, 256, 512
+S = E * C
+P = 128
+M_BLOCKS = N // P
+
+FLOPS = 2 * K * N * S
+
+F32 = mybir.dt.float32
+BF16 = mybir.dt.bfloat16
+I32 = mybir.dt.int32
+U32 = mybir.dt.uint32
+U16 = mybir.dt.uint16
+U8 = mybir.dt.uint8
+FP8X4 = mybir.dt.float8_e4m3fn_x4
+MULT = mybir.AluOpType.mult
+RELU = mybir.ActivationFunctionType.Relu
+SQUARE = mybir.ActivationFunctionType.Square
+
+CHUNKS = (
+    ((0, 1024, 0), (1024, 2048, 384), (2048, 3072, 512)),
+    ((0, 1024, 0), (1024, 2048, 384), (2048, 2560, 192), (2560, 3072, 320)),
+)
+PIECE = 512
+GATHERS = (((0, 1024), (1024, 2048)), ((0, 512), (512, 1024), (1024, 2048)))
+QUANTISE = ((0, 512), (512, 1024), (1024, 2048))
+SCATTERS = (((0, 512), (512, 1024), (1024, 2048)),) + (((0, 1024), (1024, 2048)),) * 3
+
+
+def tile_routed_moe_kernel(tc, xT, w_words, w_scales, b, gate, offs, out):
+    nc = tc.nc
+    with ExitStack() as ctx:
+        held = ctx.enter_context(tc.tile_pool(name="held", bufs=1))
+        psum = ctx.enter_context(tc.psum_pool(name="psum", bufs=8))
+
+        offsets = held.tile([P, S // 16], U16, name="offsets")
+        nc.sync.dma_start(offsets[:], offs)
+
+        w_sc = held.tile([P, E, N], U8, name="w_sc", align_bytes=64)
+        nc.gpsimd.memset(w_sc[:].rearrange("p e n -> p (e n)").bitcast(I32), 0)
+        windows = []
+        for m in range(M_BLOCKS):
+            window = held.tile([P, T], F32, name=f"window{m}")
+            (nc.vector if m < 2 else nc.gpsimd).memset(window[:], 0.0)
+            windows.append(window)
+
+        x_view = xT.rearrange("(p u v) n -> p u v n", u=2, v=2)
+        grouped = held.tile([P, S * 4], BF16, name="grouped", align_bytes=64)
+        words = grouped[:].bitcast(U32).rearrange("p (n u) -> p n u", u=2)
+        for u in range(2):
+            raw = held.tile([P, 2, T], F32, name=f"raw{u}")
+            pairs = held.tile([P, T * 2], BF16, name=f"pairs{u}", align_bytes=64)
+            paired = pairs[:].rearrange("p (n v) -> p n v", v=2)
+            for first, last, by_vector in CHUNKS[u]:
+                nc.sync.dma_start(raw[:, :, first:last], x_view[:, u, :, first:last])
+                cut = last - by_vector
+                if by_vector:
+                    nc.vector.tensor_copy(paired[:, cut:last, :], raw[:, :, cut:last].rearrange("p v n -> p n v"))
+                nc.scalar.copy(paired[:, first:cut, :], raw[:, :, first:cut].rearrange("p v n -> p n v"))
+            for a, z in GATHERS[u]:
+                nc.vector.tensor_copy(words[:, a:z, u], pairs[:].bitcast(U32).indirect(offsets[:, a // 16 : z // 16]))
+
+        bias = held.tile([P, M_BLOCKS, E], F32, name="bias")
+        nc.sync.dma_start(bias[:], b.rearrange("(m p) e -> p m e", p=P))
+        for q in range(4):
+            nc.sync.dma_start(
+                w_sc[32 * q : 32 * q + 4, :, :].bitcast(I32),
+                w_scales[:, 0, 4 * q : 4 * q + 4, :].rearrange("e q n -> q e n").bitcast(I32),
+            )
+        w = held.tile([P, E, N], I32, name="w", align_bytes=64)
+        w_view = w_words.rearrange("e a p n r -> p (e a) (n r)").bitcast(I32)
+        nc.sync.dma_start(w[:, 0:2, :], w_view[:, 0:2, :])
+        gates = [held.tile([P, S], F32, name=f"gate{m}") for m in range(M_BLOCKS)]
+        nc.sync.dma_start(w[:, 2:E, :], w_view[:, 2:E, :])
+        for m in range(M_BLOCKS):
+            nc.sync.dma_start(gates[m][:], gate[m * P : (m + 1) * P, :])
+
+        codes = held.tile([P, S], U32, name="codes", align_bytes=64)
+        scales = held.tile([P, S], U8, name="scales", align_bytes=64)
+        for a, z in QUANTISE:
+            nc.vector.quantize_mx(out=codes[:, a:z].bitcast(FP8X4), scales=scales[:, a:z], in_=grouped[:, 4 * a : 4 * z])
+
+        for m in range(M_BLOCKS):
+            features = slice(m * P, (m + 1) * P)
+            y = held.tile([P, S], F32, name=f"y{m}")
+            for i in range(S // PIECE):
+                acc = psum.tile([P, PIECE], F32, name="acc")
+                for h in range(PIECE // C):
+                    e = i * (PIECE // C) + h
+                    slots = slice(e * C, (e + 1) * C)
+                    nc.tensor.matmul_mx(
+                        out=acc[:, h * C : (h + 1) * C],
+                        lhsT=w[:, e, features].bitcast(FP8X4),
+                        lhsT_scale=w_sc[:, e, features],
+                        rhs=codes[:, slots].bitcast(FP8X4),
+                        rhs_scale=scales[:, slots],
+                        start=True,
+                        stop=True,
+                    )
+                    nc.scalar.activation(y[:, slots], acc[:, h * C : (h + 1) * C], RELU, bias=bias[:, m, e : e + 1], scale=1.0)
+                cols = slice(i * PIECE, (i + 1) * PIECE)
+                nc.scalar.activation(y[:, cols], y[:, cols], SQUARE)
+            for a, z in SCATTERS[m]:
+                nc.vector.tensor_tensor(windows[m][:].indirect(offsets[:, a // 16 : z // 16]), y[:, a:z], gates[m][:, a:z], MULT)
+            nc.sync.dma_start(out[features, :], windows[m][:])

@@ -17,12 +17,13 @@ U16 = mybir.dt.uint16
 U8 = mybir.dt.uint8
 FP8X4 = mybir.dt.float8_e4m3fn_x4
 MULT = mybir.AluOpType.mult
+COPY = mybir.ActivationFunctionType.Copy
 RELU = mybir.ActivationFunctionType.Relu
 SQUARE = mybir.ActivationFunctionType.Square
 
 CHUNKS = (
-    ((0, 1024, 0), (1024, 2048, 384), (2048, 3072, 512)),
-    ((0, 1024, 0), (1024, 2048, 384), (2048, 2560, 192), (2560, 3072, 320)),
+    ((0, 1024, 0), (1024, 2048, 512), (2048, 2560, 320), (2560, 3072, 320)),
+    ((0, 1024, 0), (1024, 2048, 0), (2048, 2560, 320), (2560, 3072, 320)),
 )
 PIECE = 512
 GATHERS = (((0, 1024), (1024, 2048)), ((0, 512), (512, 1024), (1024, 2048)))
@@ -41,10 +42,15 @@ def tile_routed_moe_kernel(tc, xT, w_words, w_scales, b, gate, offs, out):
 
         w_sc = held.tile([P, E, N], U8, name="w_sc", align_bytes=64)
         nc.gpsimd.memset(w_sc[:].rearrange("p e n -> p (e n)").bitcast(I32), 0)
+        zero = held.tile([P, 1], F32, name="zero")
+        nc.vector.memset(zero[:], 0.0)
         windows = []
         for m in range(M_BLOCKS):
             window = held.tile([P, T], F32, name=f"window{m}")
-            (nc.vector if m < 2 else nc.gpsimd).memset(window[:], 0.0)
+            if m < M_BLOCKS - 1:
+                nc.vector.memset(window[:], 0.0)
+            else:
+                nc.scalar.activation(window[:], zero[:].to_broadcast([P, T]), COPY)
             windows.append(window)
 
         x_view = xT.rearrange("(p u v) n -> p u v n", u=2, v=2)
@@ -63,19 +69,20 @@ def tile_routed_moe_kernel(tc, xT, w_words, w_scales, b, gate, offs, out):
             for a, z in GATHERS[u]:
                 nc.vector.tensor_copy(words[:, a:z, u], pairs[:].bitcast(U32).indirect(offsets[:, a // 16 : z // 16]))
 
-        bias = held.tile([P, M_BLOCKS, E], F32, name="bias")
-        nc.sync.dma_start(bias[:], b.rearrange("(m p) e -> p m e", p=P))
+        w = held.tile([P, E, N], I32, name="w", align_bytes=64)
+        w_view = w_words.rearrange("e a p n r -> p (e a) (n r)").bitcast(I32)
+        nc.sync.dma_start(w[:, 0:2, :], w_view[:, 0:2, :])
         for q in range(4):
             nc.sync.dma_start(
                 w_sc[32 * q : 32 * q + 4, :, :].bitcast(I32),
                 w_scales[:, 0, 4 * q : 4 * q + 4, :].rearrange("e q n -> q e n").bitcast(I32),
             )
-        w = held.tile([P, E, N], I32, name="w", align_bytes=64)
-        w_view = w_words.rearrange("e a p n r -> p (e a) (n r)").bitcast(I32)
-        nc.sync.dma_start(w[:, 0:2, :], w_view[:, 0:2, :])
+        bias = held.tile([P, M_BLOCKS, E], F32, name="bias")
+        nc.sync.dma_start(bias[:], b.rearrange("(m p) e -> p m e", p=P))
         gates = [held.tile([P, S], F32, name=f"gate{m}") for m in range(M_BLOCKS)]
+        nc.sync.dma_start(gates[0][:], gate[0:P, :])
         nc.sync.dma_start(w[:, 2:E, :], w_view[:, 2:E, :])
-        for m in range(M_BLOCKS):
+        for m in range(1, M_BLOCKS):
             nc.sync.dma_start(gates[m][:], gate[m * P : (m + 1) * P, :])
 
         codes = held.tile([P, S], U32, name="codes", align_bytes=64)

@@ -22,19 +22,20 @@ RELU = mybir.ActivationFunctionType.Relu
 SQUARE = mybir.ActivationFunctionType.Square
 
 CHUNKS = (
-    ((0, 1024, 0), (1024, 2048, 512), (2048, 2560, 320), (2560, 3072, 320)),
-    ((0, 1024, 0), (1024, 2048, 0), (2048, 2560, 320), (2560, 3072, 320)),
+    ((0, 1024, 0), (1024, 2048, 640), (2048, 2560, 320), (2560, 3072, 320)),
+    ((0, 512, 0), (512, 1536, 0), (1536, 2560, 384), (2560, 3072, 352)),
 )
 PIECE = 512
-GATHERS = (((0, 1024), (1024, 2048)), ((0, 512), (512, 1024), (1024, 2048)))
-QUANTISE = ((0, 512), (512, 1024), (1024, 2048))
-SCATTERS = (((0, 512), (512, 1024), (1024, 2048)),) + (((0, 1024), (1024, 2048)),) * 3
+HALF = S // 2
+SCATTERS = (((0, 512), (512, 1024), (1024, 2048)),) * 2 + (((0, 1024), (1024, 2048)),) * 2
 
 
 def tile_routed_moe_kernel(tc, xT, w_words, w_scales, b, gate, offs, out):
     nc = tc.nc
     with ExitStack() as ctx:
         held = ctx.enter_context(tc.tile_pool(name="held", bufs=1))
+        later = ctx.enter_context(tc.tile_pool(name="later", bufs=1))
+        turn = ctx.enter_context(tc.tile_pool(name="turn", bufs=1))
         psum = ctx.enter_context(tc.psum_pool(name="psum", bufs=8))
 
         offsets = held.tile([P, S // 16], U16, name="offsets")
@@ -54,8 +55,9 @@ def tile_routed_moe_kernel(tc, xT, w_words, w_scales, b, gate, offs, out):
             windows.append(window)
 
         x_view = xT.rearrange("(p u v) n -> p u v n", u=2, v=2)
-        grouped = held.tile([P, S * 4], BF16, name="grouped", align_bytes=64)
-        words = grouped[:].bitcast(U32).rearrange("p (n u) -> p n u", u=2)
+        grouped_a = turn.tile([P, HALF * 4], BF16, name="grouped_a", tag="turn", align_bytes=64)
+        words_a = grouped_a[:].bitcast(U32).rearrange("p (n u) -> p n u", u=2)
+        tables = []
         for u in range(2):
             raw = held.tile([P, 2, T], F32, name=f"raw{u}")
             pairs = held.tile([P, T * 2], BF16, name=f"pairs{u}", align_bytes=64)
@@ -66,8 +68,12 @@ def tile_routed_moe_kernel(tc, xT, w_words, w_scales, b, gate, offs, out):
                 if by_vector:
                     nc.vector.tensor_copy(paired[:, cut:last, :], raw[:, :, cut:last].rearrange("p v n -> p n v"))
                 nc.scalar.copy(paired[:, first:cut, :], raw[:, :, first:cut].rearrange("p v n -> p n v"))
-            for a, z in GATHERS[u]:
-                nc.vector.tensor_copy(words[:, a:z, u], pairs[:].bitcast(U32).indirect(offsets[:, a // 16 : z // 16]))
+            table = pairs[:].bitcast(U32)
+            nc.vector.tensor_copy(words_a[:, :, u], table.indirect(offsets[:, : HALF // 16]))
+            tables.append(table)
+            if u == 0:
+                plain0 = held.tile([P, HALF], U32, name="plain0", align_bytes=64)
+                nc.vector.tensor_copy(plain0[:], table.indirect(offsets[:, HALF // 16 :]))
 
         w = held.tile([P, E, N], I32, name="w", align_bytes=64)
         w_view = w_words.rearrange("e a p n r -> p (e a) (n r)").bitcast(I32)
@@ -87,29 +93,60 @@ def tile_routed_moe_kernel(tc, xT, w_words, w_scales, b, gate, offs, out):
 
         codes = held.tile([P, S], U32, name="codes", align_bytes=64)
         scales = held.tile([P, S], U8, name="scales", align_bytes=64)
-        for a, z in QUANTISE:
-            nc.vector.quantize_mx(out=codes[:, a:z].bitcast(FP8X4), scales=scales[:, a:z], in_=grouped[:, 4 * a : 4 * z])
+        ys = [held.tile([P, S], F32, name=f"y{m}") for m in range(M_BLOCKS)]
 
-        for m in range(M_BLOCKS):
+        def quantise(a, z, source):
+            nc.vector.quantize_mx(out=codes[:, a:z].bitcast(FP8X4), scales=scales[:, a:z], in_=source)
+
+        early = later.tile([P, HALF], F32, name="early", tag="later", align_bytes=64)
+
+        def hidden(m, i, y):
             features = slice(m * P, (m + 1) * P)
-            y = held.tile([P, S], F32, name=f"y{m}")
-            for i in range(S // PIECE):
-                acc = psum.tile([P, PIECE], F32, name="acc")
-                for h in range(PIECE // C):
-                    e = i * (PIECE // C) + h
-                    slots = slice(e * C, (e + 1) * C)
-                    nc.tensor.matmul_mx(
-                        out=acc[:, h * C : (h + 1) * C],
-                        lhsT=w[:, e, features].bitcast(FP8X4),
-                        lhsT_scale=w_sc[:, e, features],
-                        rhs=codes[:, slots].bitcast(FP8X4),
-                        rhs_scale=scales[:, slots],
-                        start=True,
-                        stop=True,
-                    )
-                    nc.scalar.activation(y[:, slots], acc[:, h * C : (h + 1) * C], RELU, bias=bias[:, m, e : e + 1], scale=1.0)
-                cols = slice(i * PIECE, (i + 1) * PIECE)
-                nc.scalar.activation(y[:, cols], y[:, cols], SQUARE)
-            for a, z in SCATTERS[m]:
-                nc.vector.tensor_tensor(windows[m][:].indirect(offsets[:, a // 16 : z // 16]), y[:, a:z], gates[m][:, a:z], MULT)
-            nc.sync.dma_start(out[features, :], windows[m][:])
+            acc = psum.tile([P, PIECE], F32, name="acc")
+            for h in range(PIECE // C):
+                e = i * (PIECE // C) + h
+                slots = slice(e * C, (e + 1) * C)
+                nc.tensor.matmul_mx(
+                    out=acc[:, h * C : (h + 1) * C],
+                    lhsT=w[:, e, features].bitcast(FP8X4),
+                    lhsT_scale=w_sc[:, e, features],
+                    rhs=codes[:, slots].bitcast(FP8X4),
+                    rhs_scale=scales[:, slots],
+                    start=True,
+                    stop=True,
+                )
+                nc.scalar.activation(y[:, slots], acc[:, h * C : (h + 1) * C], RELU, bias=bias[:, m, e : e + 1], scale=1.0)
+            cols = slice(i * PIECE, (i + 1) * PIECE)
+            nc.scalar.activation(ys[m][:, cols], y[:, cols], SQUARE)
+
+        def scatter(m, a, z):
+            nc.vector.tensor_tensor(windows[m][:].indirect(offsets[:, a // 16 : z // 16]), ys[m][:, a:z], gates[m][:, a:z], MULT)
+
+        for i in range(2):
+            quantise(i * PIECE, (i + 1) * PIECE, grouped_a[:, 4 * i * PIECE : 4 * (i + 1) * PIECE])
+        for i in range(2):
+            hidden(0, i, early)
+        plain1 = turn.tile([P, HALF], U32, name="plain1", tag="turn", align_bytes=64)
+        nc.vector.tensor_copy(plain1[:], tables[1].indirect(offsets[:, HALF // 16 :]))
+        grouped_b = later.tile([P, HALF * 4], BF16, name="grouped_b", tag="later", align_bytes=64)
+        words_b = grouped_b[:].rearrange("p (n u v) -> p n u v", u=2, v=2)
+        for u, plain in enumerate((plain0, plain1)):
+            nc.scalar.copy(words_b[:, :, u, :], plain[:].bitcast(BF16).rearrange("p (n v) -> p n v", v=2))
+        for i in range(2):
+            scatter(0, i * PIECE, (i + 1) * PIECE)
+        for i in range(2):
+            hidden(1, i, ys[1])
+        quantise(HALF, S, grouped_b[:])
+        for i in range(2):
+            scatter(1, i * PIECE, (i + 1) * PIECE)
+        for m in range(2):
+            for i in range(2, 4):
+                hidden(m, i, ys[m])
+            scatter(m, HALF, S)
+            nc.sync.dma_start(out[m * P : (m + 1) * P, :], windows[m][:])
+        for m in range(2, M_BLOCKS):
+            for i in range(4):
+                hidden(m, i, ys[m])
+            for a in (0, HALF):
+                scatter(m, a, a + HALF)
+            nc.sync.dma_start(out[m * P : (m + 1) * P, :], windows[m][:])

@@ -86,9 +86,11 @@ def tile_routed_moe_kernel(tc, xT, w_words, w_scales, b, gate, offs, out):
         bias = held.tile([P, M_BLOCKS, E], F32, name="bias")
         nc.sync.dma_start(bias[:], b.rearrange("(m p) e -> p m e", p=P))
         gates = [held.tile([P, S], F32, name=f"gate{m}") for m in range(M_BLOCKS)]
-        nc.sync.dma_start(gates[0][:], gate[0:P, :])
-        nc.sync.dma_start(w[:, 2:E, :], w_view[:, 2:E, :])
-        for m in range(1, M_BLOCKS):
+        nc.sync.dma_start(w[:, 2:4, :], w_view[:, 2:4, :])
+        for m in range(2):
+            nc.sync.dma_start(gates[m][:], gate[m * P : (m + 1) * P, :])
+        nc.sync.dma_start(w[:, 4:E, :], w_view[:, 4:E, :])
+        for m in range(2, M_BLOCKS):
             nc.sync.dma_start(gates[m][:], gate[m * P : (m + 1) * P, :])
 
         codes = held.tile([P, S], U32, name="codes", align_bytes=64)
@@ -98,7 +100,7 @@ def tile_routed_moe_kernel(tc, xT, w_words, w_scales, b, gate, offs, out):
         def quantise(a, z, source):
             nc.vector.quantize_mx(out=codes[:, a:z].bitcast(FP8X4), scales=scales[:, a:z], in_=source)
 
-        early = later.tile([P, HALF], F32, name="early", tag="later", align_bytes=64)
+        early = later.tile([P, 2, HALF], F32, name="early", tag="later", align_bytes=64)
 
         def hidden(m, i, y):
             features = slice(m * P, (m + 1) * P)
@@ -125,7 +127,9 @@ def tile_routed_moe_kernel(tc, xT, w_words, w_scales, b, gate, offs, out):
         for i in range(2):
             quantise(i * PIECE, (i + 1) * PIECE, grouped_a[:, 4 * i * PIECE : 4 * (i + 1) * PIECE])
         for i in range(2):
-            hidden(0, i, early)
+            hidden(0, i, early[:, 0, :])
+        for i in range(2):
+            hidden(1, i, early[:, 1, :])
         plain1 = turn.tile([P, HALF], U32, name="plain1", tag="turn", align_bytes=64)
         nc.vector.tensor_copy(plain1[:], tables[1].indirect(offsets[:, HALF // 16 :]))
         grouped_b = later.tile([P, HALF * 4], BF16, name="grouped_b", tag="later", align_bytes=64)
@@ -134,17 +138,18 @@ def tile_routed_moe_kernel(tc, xT, w_words, w_scales, b, gate, offs, out):
             nc.scalar.copy(words_b[:, :, u, :], plain[:].bitcast(BF16).rearrange("p (n v) -> p n v", v=2))
         for i in range(2):
             scatter(0, i * PIECE, (i + 1) * PIECE)
+        scatter(1, 0, HALF)
         for i in range(2):
-            hidden(1, i, ys[1])
+            hidden(2, i, ys[2])
         quantise(HALF, S, grouped_b[:])
         for i in range(2):
-            scatter(1, i * PIECE, (i + 1) * PIECE)
-        for m in range(2):
+            scatter(2, i * PIECE, (i + 1) * PIECE)
+        for m in range(3):
             for i in range(2, 4):
                 hidden(m, i, ys[m])
             scatter(m, HALF, S)
             nc.sync.dma_start(out[m * P : (m + 1) * P, :], windows[m][:])
-        for m in range(2, M_BLOCKS):
+        for m in range(3, M_BLOCKS):
             for i in range(4):
                 hidden(m, i, ys[m])
             for a in (0, HALF):

from contextlib import ExitStack

import concourse.mybir as mybir

K, T, E, C, N = 512, 3072, 8, 256, 512
S = E * C
P = 128
M_BLOCKS = N // P

FLOPS = 2 * K * N * S

F32 = mybir.dt.float32
BF16 = mybir.dt.bfloat16
I32 = mybir.dt.int32
U32 = mybir.dt.uint32
U16 = mybir.dt.uint16
U8 = mybir.dt.uint8
FP8X4 = mybir.dt.float8_e4m3fn_x4
MULT = mybir.AluOpType.mult
COPY = mybir.ActivationFunctionType.Copy
RELU = mybir.ActivationFunctionType.Relu
SQUARE = mybir.ActivationFunctionType.Square

CHUNKS = (
    ((0, 1024, 0), (1024, 2048, 640), (2048, 2560, 320), (2560, 3072, 320)),
    ((0, 512, 0), (512, 1536, 0), (1536, 2560, 384), (2560, 3072, 352)),
)
PIECE = 512
HALF = S // 2
SCATTERS = (((0, 512), (512, 1024), (1024, 2048)),) * 2 + (((0, 1024), (1024, 2048)),) * 2


def tile_routed_moe_kernel(tc, xT, w_words, w_scales, b, gate, offs, out):
    nc = tc.nc
    with ExitStack() as ctx:
        held = ctx.enter_context(tc.tile_pool(name="held", bufs=1))
        later = ctx.enter_context(tc.tile_pool(name="later", bufs=1))
        turn = ctx.enter_context(tc.tile_pool(name="turn", bufs=1))
        psum = ctx.enter_context(tc.psum_pool(name="psum", bufs=8))

        offsets = held.tile([P, S // 16], U16, name="offsets")
        nc.sync.dma_start(offsets[:], offs)

        w_sc = held.tile([P, E, N], U8, name="w_sc", align_bytes=64)
        nc.gpsimd.memset(w_sc[:].rearrange("p e n -> p (e n)").bitcast(I32), 0)
        zero = held.tile([P, 1], F32, name="zero")
        nc.vector.memset(zero[:], 0.0)
        windows = []
        for m in range(M_BLOCKS):
            window = held.tile([P, T], F32, name=f"window{m}")
            if m < M_BLOCKS - 1:
                nc.vector.memset(window[:], 0.0)
            else:
                nc.scalar.activation(window[:], zero[:].to_broadcast([P, T]), COPY)
            windows.append(window)

        x_view = xT.rearrange("(p u v) n -> p u v n", u=2, v=2)
        grouped_a = turn.tile([P, HALF * 4], BF16, name="grouped_a", tag="turn", align_bytes=64)
        words_a = grouped_a[:].bitcast(U32).rearrange("p (n u) -> p n u", u=2)
        tables = []
        for u in range(2):
            raw = held.tile([P, 2, T], F32, name=f"raw{u}")
            pairs = held.tile([P, T * 2], BF16, name=f"pairs{u}", align_bytes=64)
            paired = pairs[:].rearrange("p (n v) -> p n v", v=2)
            for first, last, by_vector in CHUNKS[u]:
                nc.sync.dma_start(raw[:, :, first:last], x_view[:, u, :, first:last])
                cut = last - by_vector
                if by_vector:
                    nc.vector.tensor_copy(paired[:, cut:last, :], raw[:, :, cut:last].rearrange("p v n -> p n v"))
                nc.scalar.copy(paired[:, first:cut, :], raw[:, :, first:cut].rearrange("p v n -> p n v"))
            table = pairs[:].bitcast(U32)
            nc.vector.tensor_copy(words_a[:, :, u], table.indirect(offsets[:, : HALF // 16]))
            tables.append(table)
            if u == 0:
                plain0 = held.tile([P, HALF], U32, name="plain0", align_bytes=64)
                nc.vector.tensor_copy(plain0[:], table.indirect(offsets[:, HALF // 16 :]))

        w = held.tile([P, E, N], I32, name="w", align_bytes=64)
        w_view = w_words.rearrange("e a p n r -> p (e a) (n r)").bitcast(I32)
        nc.sync.dma_start(w[:, 0:2, :], w_view[:, 0:2, :])
        for q in range(4):
            nc.sync.dma_start(
                w_sc[32 * q : 32 * q + 4, :, :].bitcast(I32),
                w_scales[:, 0, 4 * q : 4 * q + 4, :].rearrange("e q n -> q e n").bitcast(I32),
            )
        bias = held.tile([P, M_BLOCKS, E], F32, name="bias")
        nc.sync.dma_start(bias[:], b.rearrange("(m p) e -> p m e", p=P))
        gates = [held.tile([P, S], F32, name=f"gate{m}") for m in range(M_BLOCKS)]
        nc.sync.dma_start(w[:, 2:4, :], w_view[:, 2:4, :])
        for m in range(2):
            nc.sync.dma_start(gates[m][:], gate[m * P : (m + 1) * P, :])
        nc.sync.dma_start(w[:, 4:E, :], w_view[:, 4:E, :])
        for m in range(2, M_BLOCKS):
            nc.sync.dma_start(gates[m][:], gate[m * P : (m + 1) * P, :])

        codes = held.tile([P, S], U32, name="codes", align_bytes=64)
        scales = held.tile([P, S], U8, name="scales", align_bytes=64)
        ys = [held.tile([P, S], F32, name=f"y{m}") for m in range(M_BLOCKS)]

        def quantise(a, z, source):
            nc.vector.quantize_mx(out=codes[:, a:z].bitcast(FP8X4), scales=scales[:, a:z], in_=source)

        early = later.tile([P, 2, HALF], F32, name="early", tag="later", align_bytes=64)

        def hidden(m, i, y):
            features = slice(m * P, (m + 1) * P)
            acc = psum.tile([P, PIECE], F32, name="acc")
            for h in range(PIECE // C):
                e = i * (PIECE // C) + h
                slots = slice(e * C, (e + 1) * C)
                nc.tensor.matmul_mx(
                    out=acc[:, h * C : (h + 1) * C],
                    lhsT=w[:, e, features].bitcast(FP8X4),
                    lhsT_scale=w_sc[:, e, features],
                    rhs=codes[:, slots].bitcast(FP8X4),
                    rhs_scale=scales[:, slots],
                    start=True,
                    stop=True,
                )
                nc.scalar.activation(y[:, slots], acc[:, h * C : (h + 1) * C], RELU, bias=bias[:, m, e : e + 1], scale=1.0)
            cols = slice(i * PIECE, (i + 1) * PIECE)
            nc.scalar.activation(ys[m][:, cols], y[:, cols], SQUARE)

        def scatter(m, a, z):
            nc.vector.tensor_tensor(windows[m][:].indirect(offsets[:, a // 16 : z // 16]), ys[m][:, a:z], gates[m][:, a:z], MULT)

        for i in range(2):
            quantise(i * PIECE, (i + 1) * PIECE, grouped_a[:, 4 * i * PIECE : 4 * (i + 1) * PIECE])
        for i in range(2):
            hidden(0, i, early[:, 0, :])
        for i in range(2):
            hidden(1, i, early[:, 1, :])
        plain1 = turn.tile([P, HALF], U32, name="plain1", tag="turn", align_bytes=64)
        nc.vector.tensor_copy(plain1[:], tables[1].indirect(offsets[:, HALF // 16 :]))
        grouped_b = later.tile([P, HALF * 4], BF16, name="grouped_b", tag="later", align_bytes=64)
        words_b = grouped_b[:].rearrange("p (n u v) -> p n u v", u=2, v=2)
        for u, plain in enumerate((plain0, plain1)):
            nc.scalar.copy(words_b[:, :, u, :], plain[:].bitcast(BF16).rearrange("p (n v) -> p n v", v=2))
        for i in range(2):
            scatter(0, i * PIECE, (i + 1) * PIECE)
        scatter(1, 0, HALF)
        for i in range(2):
            hidden(2, i, ys[2])
        quantise(HALF, S, grouped_b[:])
        for i in range(2):
            scatter(2, i * PIECE, (i + 1) * PIECE)
        for m in range(3):
            for i in range(2, 4):
                hidden(m, i, ys[m])
            scatter(m, HALF, S)
            nc.sync.dma_start(out[m * P : (m + 1) * P, :], windows[m][:])
        for m in range(3, M_BLOCKS):
            for i in range(4):
                hidden(m, i, ys[m])
            for a in (0, HALF):
                scatter(m, a, a + HALF)
            nc.sync.dma_start(out[m * P : (m + 1) * P, :], windows[m][:])
